import numpy as np
import ml_dtypes


def mxq(x, axis, fmt="e4m3"):
    dtype, down = {"e4m3": (ml_dtypes.float8_e4m3fn, 7), "e5m2": (ml_dtypes.float8_e5m2, 14)}[fmt]
    v = np.moveaxis(np.asarray(x, np.float32).astype(ml_dtypes.bfloat16).astype(np.float64), axis, -1)
    blocks = v.reshape(v.shape[:-1] + (-1, 32))
    amax = np.abs(blocks).max(-1, keepdims=True)
    byte = np.maximum(np.where(amax > 0, np.frexp(amax)[1] - 1 + 127, 0) - down, 1)
    scale = np.exp2(byte - 127.0)
    codes = (blocks / scale).astype(np.float32).astype(dtype).astype(np.float64)
    return np.moveaxis((codes * scale).reshape(v.shape), -1, axis)


WIDE = False


def mx_kscale(k):
    if not WIDE:
        return np.ones(k)
    levels = np.array([10, -10, 5, -5, 0])
    if k % 512:
        return np.exp2(np.random.permutation(np.resize(levels, k // 32))).repeat(32)
    a = np.empty((k // 512, 16))
    for p in range(k // 512):
        a[p, :8] = np.random.permutation(np.resize(levels, 8))
        for g in range(8):
            far = levels[np.abs(levels - a[p, g]) >= 10]
            a[p, g + 8] = far[np.random.randint(len(far))]
    return np.exp2(a.ravel()).repeat(32)


def f64(x):
    return np.asarray(x).astype(np.float64)


def striped(idx):
    return np.tile(np.asarray(idx).reshape(-1, 16).T, (8, 1)).astype(np.uint16)


def unstriped(offs):
    return offs[:16].T.reshape(-1).astype(np.int64)


E2M1 = np.array([0.0, 0.5, 1.0, 1.5, 2.0, 3.0, 4.0, 6.0, -0.0, -0.5, -1.0, -1.5, -2.0, -3.0, -4.0, -6.0])


def pack_weight(w, fmt):
    k, n = w.shape
    w = f64(np.asarray(w, np.float32).astype(ml_dtypes.bfloat16)).reshape(k // 32, 32, n)
    amax = np.abs(w).max(1)
    if fmt == "e4m3":
        byte = np.frexp(amax)[1] - 1 + 127 - 7
    else:
        mant, ex = np.frexp(amax / 6.0)
        byte = np.where(mant > 0.5, ex, ex - 1) + 127
    byte = np.clip(np.where(amax > 0, byte, 1), 1, 254)
    scaled = (w * np.exp2(127.0 - byte)[:, None, :]).reshape(k, n).astype(np.float32)
    by_word = np.ascontiguousarray(scaled.reshape(k // 512, 128, 4, n).transpose(0, 1, 3, 2))
    if fmt == "e4m3":
        words = by_word.astype(ml_dtypes.float8_e4m3fn).view(np.uint8)
    else:
        c = by_word.astype(ml_dtypes.float4_e2m1fn).view(np.uint8) & 0xF
        words = (c[..., 0::2] | (c[..., 1::2] << 4)).reshape(k // 512, 128, 2 * n)
    return np.ascontiguousarray(words), np.ascontiguousarray(byte.astype(np.uint8).reshape(k // 512, 16, n))


def unpack_weight(words, scales, fmt):
    g, _, n = scales.shape
    words = np.ascontiguousarray(words).reshape(g, 128, n, -1)
    if fmt == "e4m3":
        vals = words.view(ml_dtypes.float8_e4m3fn).astype(np.float64)
    else:
        nib = np.empty((g, 128, n, 4), np.uint8)
        nib[..., 0::2] = words & 0xF
        nib[..., 1::2] = words >> 4
        vals = E2M1[nib]
    vals = vals * np.repeat(np.exp2(scales.astype(np.float64) - 127.0), 8, axis=1)[..., None]
    return vals.transpose(0, 1, 3, 2).reshape(g * 512, n)


B, N, T, D, DV, NQ = 2, 512, 2048, 512, 128, 128
CAP = 2.0


def setup_inputs():
    n = np.random.standard_normal
    seg = T // B
    idx = np.concatenate([b * seg + np.random.permutation(seg)[:N] for b in range(B)])
    s = mx_kscale(D)[:, None]
    u = np.ones(T)
    u[idx] = mx_kscale(B * N)
    r = np.random.uniform(0.5, 2.0, T)
    k = n((D, T)) / s
    v = n((DV, T)) / (u * r)
    kp = pack_weight(k, "e4m3")
    return {
        "qT": (n((B, D, NQ)) * s * (1.00 / np.sqrt(D))).astype(np.float32),
        "k_words": kp[0],
        "k_scales": kp[1],
        "vT": v.astype(np.float32),
        "vs": np.tile(u * r, (128, 1)).astype(np.float32),
        "sink": (2.0 + 3.0 * n((B, NQ, 1))).astype(np.float32),
        "offs": striped(idx),
    }


def reference(qT, k_words, k_scales, vT, vs, sink, offs):
    idx = unstriped(offs)
    k = unpack_weight(k_words, k_scales, "e4m3")
    v = f64(vT)
    pick = lambda x: x[:, idx].reshape(x.shape[0], B, N).transpose(1, 0, 2)
    q = f64(qT)
    score = mxq(q, 1, "e4m3").transpose(0, 2, 1) @ pick(k)
    score = CAP * np.tanh(score / CAP)
    m = np.maximum(score.max(-1, keepdims=True), f64(sink))
    p = np.exp(score - m)
    total = p.sum(-1, keepdims=True) + np.exp(f64(sink) - m)
    w = p * pick(f64(vs))[:, :1, :]
    y = mxq(w, 2, "e4m3") @ mxq(pick(v).transpose(0, 2, 1), 1, "e4m3")
    y = y / total
    return y

@@ -1,0 +1,201 @@
+from contextlib import ExitStack
+
+import concourse.mybir as mybir
+from concourse.masks import make_identity
+
+B, N, T, D, DV, NQ = 2, 512, 2048, 512, 128, 128
+CAP = 2.0
+FLOPS = 2 * B * NQ * N * (D + DV)
+
+F32 = mybir.dt.float32
+BF16 = mybir.dt.bfloat16
+I32 = mybir.dt.int32
+U32 = mybir.dt.uint32
+U16 = mybir.dt.uint16
+U8 = mybir.dt.uint8
+FP8X4 = mybir.dt.float8_e4m3fn_x4
+ACT = mybir.ActivationFunctionType
+ALU = mybir.AluOpType
+
+P = 128
+PACK = 4
+SEG = T // B
+COLS = N // 16
+
+
+def tile_attend_cap_sink_seg_kernel(tc, qT, k_words, k_scales, vT, vs, sink, offs, out):
+    nc = tc.nc
+    with ExitStack() as ctx:
+        keep = ctx.enter_context(tc.tile_pool(name="keep", bufs=1))
+        psum = ctx.enter_context(tc.psum_pool(name="psum", bufs=1))
+        reuse = ctx.enter_context(tc.tile_pool(name="reuse", bufs=1))
+
+        def sb(name, shape, dtype):
+            return keep.tile(shape, dtype, name=name, align_bytes=64)
+
+        def per_seq(name, shape, dtype):
+            return [sb("%s%d" % (name, b), shape, dtype) for b in range(B)]
+
+        offsets = keep.tile([P, B * COLS], U16, name="offsets")
+        kw_pool = sb("kw_pool", [P, T], U32)
+        ks_pool = sb("ks_pool", [P, T], U8)
+        v_pool = sb("v_pool", [P, T], F32)
+        vs_pool = sb("vs_pool", [P, T], F32)
+        v0_bf = sb("v0_bf", [P, SEG], BF16)
+        sink_sb = sb("sink_sb", [P, B], F32)
+        ident = sb("ident", [P, P], F32)
+        warm = sb("warm", [P, 1], F32)
+        warm_out = sb("warm_out", [P, 1], F32)
+        q_raw = sb("q_raw", [P, B, PACK, NQ], F32)
+        q_il = per_seq("q_il", [P, NQ, PACK], BF16)
+        q_codes = per_seq("q_codes", [P, NQ], U32)
+        q_scales = per_seq("q_scales", [P, NQ], U8)
+        kw = per_seq("kw", [P, N], U32)
+        ks = sb("ks", [P, B * N], U8)
+        vg = per_seq("vg", [P, N], BF16)
+        vsg = [reuse.tile([P, N], F32, name="vsg%d" % b, align_bytes=64, offset=4096 * b) for b in range(B)]
+        vs_col = per_seq("vs_col", [P, PACK], F32)
+        v_il = per_seq("v_il", [P, DV, PACK], BF16)
+        v_codes = per_seq("v_codes", [P, DV], U32)
+        v_scales = per_seq("v_scales", [P, DV], U8)
+        half = [reuse.tile([P, N + 1], F32, name="half%d" % b, align_bytes=64, offset=4096 * b) for b in range(B)]
+        negc = per_seq("negc", [P, N + 1], F32)
+        prob = per_seq("prob", [P, N + 1], F32)
+        negm = per_seq("negm", [P, 1], F32)
+        total = per_seq("total", [P, 1], F32)
+        inv = per_seq("inv", [P, 1], F32)
+        w_il = per_seq("w_il", [P, NQ, PACK], BF16)
+        w_codes = per_seq("w_codes", [P, NQ], U32)
+        w_scales = per_seq("w_scales", [P, NQ], U8)
+        res = per_seq("res", [P, DV], F32)
+
+        def seg(b):
+            return slice(b * SEG, (b + 1) * SEG)
+
+        def window(pool_tile, b):
+            return pool_tile[:, : (b + 1) * SEG].indirect(offsets[:, b * COLS : (b + 1) * COLS])
+
+        words = k_words[0].rearrange("p n t -> p (n t)")
+
+        nc.vector.memset(ks_pool[:].bitcast(I32), 0)
+        nc.vector.memset(warm[:], 0.0)
+        nc.vector.memset(vs_pool[:, :1280], 0.0)
+        nc.gpsimd.memset(vs_pool[:, 1280:], 0.0)
+        make_identity(nc, ident[:])
+
+        nc.sync.dma_start(offsets[:], offs)
+        with nc.allow_non_contiguous_dma(reason="one sink logit a partition and sequence"):
+            nc.sync.dma_start(out=sink_sb[:], in_=sink.rearrange("b q o -> q (b o)"))
+        for quad in range(4):
+            queue = nc.sync if quad < 2 else nc.scalar
+            queue.dma_start(
+                out=ks_pool[32 * quad : 32 * quad + 4, :].bitcast(I32),
+                in_=k_scales[0, 4 * quad : 4 * quad + 4, :].bitcast(I32),
+            )
+        nc.scalar.activation(warm_out[:], warm[:], ACT.Exp)
+        nc.sync.dma_start(
+            out=q_raw[:].rearrange("p b j q -> p b (j q)"),
+            in_=qT.rearrange("b (p j) q -> p b (j q)", j=PACK),
+        )
+        for b in range(B):
+            nc.sync.dma_start(
+                out=kw_pool[:, seg(b)].bitcast(I32),
+                in_=words[:, b * SEG * PACK : (b + 1) * SEG * PACK].bitcast(I32),
+            )
+        nc.sync.dma_start(out=vs_pool[0:1, :], in_=vs[0:1, :])
+        for b in range(B):
+            nc.sync.dma_start(out=v_pool[:, seg(b)], in_=vT[:, seg(b)])
+        for b in range(B):
+            nc.gpsimd.tensor_scalar(half[b][:, N : N + 1], sink_sb[:, b : b + 1], 1.0 / CAP, 0.0, ALU.mult, ALU.add)
+
+        def quantize(codes, scales, src):
+            nc.vector.quantize_mx(out=codes[:].bitcast(FP8X4), scales=scales[:], in_=src[:].rearrange("p c t -> p (c t)"))
+
+        def queries(b):
+            nc.scalar.activation(q_il[b][:], q_raw[:, b].rearrange("p j q -> p q j"), ACT.Copy)
+
+        def keys(b):
+            quantize(q_codes[b], q_scales[b], q_il[b])
+            nc.vector.tensor_copy(kw[b][:], window(kw_pool, b))
+
+        def scores(b):
+            acc = psum.tile([P, N], F32, name="acc%d" % b)
+            nc.tensor.matmul_mx(
+                out=acc[:], lhsT=q_codes[b][:].bitcast(FP8X4), lhsT_scale=q_scales[b][:],
+                rhs=kw[b][:].bitcast(FP8X4), rhs_scale=ks[:, b * N : (b + 1) * N], start=True, stop=True,
+            )
+            nc.scalar.activation(
+                half[b][:, :N].rearrange("q (t s) -> q t s", t=PACK),
+                acc[:].rearrange("q (s t) -> q t s", t=PACK),
+                ACT.Tanh, scale=1.0 / CAP,
+            )
+
+        def row_max(b):
+            nc.vector.tensor_scalar(negc[b][:], half[b][:], -CAP, None, ALU.mult, ALU.min, accum_out=negm[b][:])
+
+        p_turned = [psum.tile([P, PACK, NQ], F32, name="p_turned%d" % b) for b in range(B)]
+
+        def softmax(b):
+            nc.scalar.activation(prob[b][:], negc[b][:], ACT.Exp, bias=negm[b][:], scale=-1.0, accum_out=total[b][:])
+            for t in range(PACK):
+                nc.tensor.transpose(p_turned[b][:, t, :], prob[b][:, t * P : (t + 1) * P], ident[:])
+
+        def token_scales(b):
+            nc.vector.tensor_copy(vsg[b][:], window(vs_pool, b))
+            turned = psum.tile([P, PACK, P], F32, name="vs_turned%d" % b)
+            for t in range(PACK):
+                nc.tensor.transpose(turned[:, t, :], vsg[b][:, t::PACK], ident[:])
+            nc.scalar.copy(vs_col[b][:], turned[:, :, 0])
+
+        def values(b):
+            if b == 0:
+                nc.scalar.activation(vg[0][:], v0_bf[:].indirect(offsets[:, :COLS]), ACT.Copy)
+            else:
+                nc.vector.tensor_copy(vg[1][:], window(v_pool, 1))
+            turned = psum.tile([P, 2, DV], F32, name="v_turned%d" % b)
+            pairs = vg[b][:].bitcast(F32)
+            for u in range(2):
+                nc.tensor.transpose(turned[:, u, :], pairs[:, u::2], ident[:])
+            nc.scalar.copy(
+                v_il[b][:].rearrange("p e t -> p (e t)").bitcast(F32).rearrange("p (e u) -> p e u", u=2),
+                turned[:].rearrange("p u e -> p e u"),
+            )
+
+        def weights(b):
+            nc.vector.tensor_tensor(
+                w_il[b][:], p_turned[b][:].rearrange("p t q -> p q t"),
+                vs_col[b][:].unsqueeze(1).to_broadcast([P, NQ, PACK]), ALU.mult,
+            )
+            quantize(v_codes[b], v_scales[b], v_il[b])
+            nc.vector.reciprocal(inv[b][:], total[b][:])
+            quantize(w_codes[b], w_scales[b], w_il[b])
+
+        def finish(b):
+            y = psum.tile([P, DV], F32, name="acc%d" % b)
+            nc.tensor.matmul_mx(
+                out=y[:], lhsT=w_codes[b][:].bitcast(FP8X4), lhsT_scale=w_scales[b][:],
+                rhs=v_codes[b][:].bitcast(FP8X4), rhs_scale=v_scales[b][:], start=True, stop=True,
+            )
+            nc.scalar.activation(res[b][:], y[:], ACT.Copy, scale=inv[b][:])
+            nc.sync.dma_start(out=out[b], in_=res[b][:])
+
+        nc.vector.tensor_copy(ks[:], ks_pool[:].indirect(offsets[:]))
+        queries(0)
+        queries(1)
+        keys(0)
+        scores(0)
+        keys(1)
+        scores(1)
+        row_max(0)
+        softmax(0)
+        token_scales(0)
+        nc.scalar.activation(v0_bf[:], v_pool[:, seg(0)], ACT.Copy)
+        row_max(1)
+        softmax(1)
+        token_scales(1)
+        values(0)
+        values(1)
+        weights(0)
+        finish(0)
+        weights(1)
+        finish(1)

@@ -33,9 +33,13 @@ def tile_attend_cap_sink_seg_kernel(tc, qT, k_words, k_scales, vT, vs, sink, off
         def sb(name, shape, dtype):
             return keep.tile(shape, dtype, name=name, align_bytes=64)
 
+        def at(offset, name, shape, dtype):
+            return reuse.tile(shape, dtype, name=name, align_bytes=64, offset=offset)
+
         def per_seq(name, shape, dtype):
             return [sb("%s%d" % (name, b), shape, dtype) for b in range(B)]
 
+        KW = 0
         offsets = keep.tile([P, B * COLS], U16, name="offsets")
         kw_pool = sb("kw_pool", [P, T], U32)
         ks_pool = sb("ks_pool", [P, T], U8)
@@ -47,23 +51,23 @@ def tile_attend_cap_sink_seg_kernel(tc, qT, k_words, k_scales, vT, vs, sink, off
         warm = sb("warm", [P, 1], F32)
         warm_out = sb("warm_out", [P, 1], F32)
         q_raw = sb("q_raw", [P, B, PACK, NQ], F32)
-        q_il = per_seq("q_il", [P, NQ, PACK], BF16)
-        q_codes = per_seq("q_codes", [P, NQ], U32)
-        q_scales = per_seq("q_scales", [P, NQ], U8)
+        q_il = sb("q_il", [P, B, NQ, PACK], BF16)
+        q_codes = sb("q_codes", [P, B * NQ], U32)
+        q_scales = sb("q_scales", [P, B * NQ], U8)
         kw = per_seq("kw", [P, N], U32)
         ks = sb("ks", [P, B * N], U8)
+        half = per_seq("half", [P, N + 1], F32)
+        negc = [sb("negc0", [P, N + 1], F32), at(KW, "negc1", [P, N + 1], F32)]
+        vsg = per_seq("vsg", [P, N], F32)
         vg = per_seq("vg", [P, N], BF16)
-        vsg = [reuse.tile([P, N], F32, name="vsg%d" % b, align_bytes=64, offset=4096 * b) for b in range(B)]
         vs_col = per_seq("vs_col", [P, PACK], F32)
-        v_il = per_seq("v_il", [P, DV, PACK], BF16)
+        v_il = [at(KW, "v_il0", [P, DV, PACK], BF16), sb("v_il1", [P, DV, PACK], BF16)]
         v_codes = per_seq("v_codes", [P, DV], U32)
         v_scales = per_seq("v_scales", [P, DV], U8)
-        half = [reuse.tile([P, N + 1], F32, name="half%d" % b, align_bytes=64, offset=4096 * b) for b in range(B)]
-        negc = per_seq("negc", [P, N + 1], F32)
         prob = per_seq("prob", [P, N + 1], F32)
         negm = per_seq("negm", [P, 1], F32)
-        total = per_seq("total", [P, 1], F32)
-        inv = per_seq("inv", [P, 1], F32)
+        total = sb("total", [P, B], F32)
+        inv = sb("inv", [P, B], F32)
         w_il = per_seq("w_il", [P, NQ, PACK], BF16)
         w_codes = per_seq("w_codes", [P, NQ], U32)
         w_scales = per_seq("w_scales", [P, NQ], U8)
@@ -77,15 +81,15 @@ def tile_attend_cap_sink_seg_kernel(tc, qT, k_words, k_scales, vT, vs, sink, off
 
         words = k_words[0].rearrange("p n t -> p (n t)")
 
-        nc.vector.memset(ks_pool[:].bitcast(I32), 0)
+        nc.vector.memset(ks_pool[:, :SEG].bitcast(I32), 0)
+        nc.gpsimd.memset(ks_pool[:, SEG:].bitcast(I32), 0)
         nc.vector.memset(warm[:], 0.0)
-        nc.vector.memset(vs_pool[:, :1280], 0.0)
-        nc.gpsimd.memset(vs_pool[:, 1280:], 0.0)
-        make_identity(nc, ident[:])
+        nc.vector.memset(ident[:], 0.0)
+        for b in range(B):
+            nc.vector.memset(vs_pool[:, seg(b)].bitcast(I32), 0)
+        make_identity(nc, ident[:], nomemset=True)
 
         nc.sync.dma_start(offsets[:], offs)
-        with nc.allow_non_contiguous_dma(reason="one sink logit a partition and sequence"):
-            nc.sync.dma_start(out=sink_sb[:], in_=sink.rearrange("b q o -> q (b o)"))
         for quad in range(4):
             queue = nc.sync if quad < 2 else nc.scalar
             queue.dma_start(
@@ -93,35 +97,48 @@ def tile_attend_cap_sink_seg_kernel(tc, qT, k_words, k_scales, vT, vs, sink, off
                 in_=k_scales[0, 4 * quad : 4 * quad + 4, :].bitcast(I32),
             )
         nc.scalar.activation(warm_out[:], warm[:], ACT.Exp)
-        nc.sync.dma_start(
-            out=q_raw[:].rearrange("p b j q -> p b (j q)"),
-            in_=qT.rearrange("b (p j) q -> p b (j q)", j=PACK),
-        )
-        for b in range(B):
+
+        def load_words(b):
             nc.sync.dma_start(
                 out=kw_pool[:, seg(b)].bitcast(I32),
                 in_=words[:, b * SEG * PACK : (b + 1) * SEG * PACK].bitcast(I32),
             )
-        nc.sync.dma_start(out=vs_pool[0:1, :], in_=vs[0:1, :])
-        for b in range(B):
-            nc.sync.dma_start(out=v_pool[:, seg(b)], in_=vT[:, seg(b)])
-        for b in range(B):
-            nc.gpsimd.tensor_scalar(half[b][:, N : N + 1], sink_sb[:, b : b + 1], 1.0 / CAP, 0.0, ALU.mult, ALU.add)
+
+        nc.sync.dma_start(
+            out=q_raw[:].rearrange("p b j q -> p b (j q)"),
+            in_=qT.rearrange("b (p j) q -> p b (j q)", j=PACK),
+        )
+        load_words(0)
+        v0_parts = (slice(0, 768), slice(768, SEG))
+        for part in v0_parts:
+            nc.sync.dma_start(out=v_pool[:, part], in_=vT[:, part])
+        nc.sync.dma_start(out=vs_pool[0:1, seg(0)], in_=vs[0:1, seg(0)])
+        load_words(1)
+        nc.sync.dma_start(out=vs_pool[0:1, seg(1)], in_=vs[0:1, seg(1)])
+        with nc.allow_non_contiguous_dma(reason="one sink logit a partition and sequence"):
+            nc.sync.dma_start(out=sink_sb[:], in_=sink.rearrange("b q o -> q (b o)"))
+        nc.sync.dma_start(out=v_pool[:, seg(1)], in_=vT[:, seg(1)])
 
         def quantize(codes, scales, src):
-            nc.vector.quantize_mx(out=codes[:].bitcast(FP8X4), scales=scales[:], in_=src[:].rearrange("p c t -> p (c t)"))
+            nc.vector.quantize_mx(out=codes[:].bitcast(FP8X4), scales=scales[:], in_=src)
+
+        def flat(tile3):
+            return tile3[:].rearrange("p c t -> p (c t)")
+
+        def sink_column(b):
+            nc.gpsimd.tensor_scalar(half[b][:, N : N + 1], sink_sb[:, b : b + 1], 1.0 / CAP, 0.0, ALU.mult, ALU.add)
 
         def queries(b):
-            nc.scalar.activation(q_il[b][:], q_raw[:, b].rearrange("p j q -> p q j"), ACT.Copy)
+            nc.scalar.activation(q_il[:, b], q_raw[:, b].rearrange("p j q -> p q j"), ACT.Copy)
 
         def keys(b):
-            quantize(q_codes[b], q_scales[b], q_il[b])
             nc.vector.tensor_copy(kw[b][:], window(kw_pool, b))
 
         def scores(b):
             acc = psum.tile([P, N], F32, name="acc%d" % b)
+            cols = slice(b * NQ, (b + 1) * NQ)
             nc.tensor.matmul_mx(
-                out=acc[:], lhsT=q_codes[b][:].bitcast(FP8X4), lhsT_scale=q_scales[b][:],
+                out=acc[:], lhsT=q_codes[:, cols].bitcast(FP8X4), lhsT_scale=q_scales[:, cols],
                 rhs=kw[b][:].bitcast(FP8X4), rhs_scale=ks[:, b * N : (b + 1) * N], start=True, stop=True,
             )
             nc.scalar.activation(
@@ -136,28 +153,27 @@ def tile_attend_cap_sink_seg_kernel(tc, qT, k_words, k_scales, vT, vs, sink, off
         p_turned = [psum.tile([P, PACK, NQ], F32, name="p_turned%d" % b) for b in range(B)]
 
         def softmax(b):
-            nc.scalar.activation(prob[b][:], negc[b][:], ACT.Exp, bias=negm[b][:], scale=-1.0, accum_out=total[b][:])
+            nc.scalar.activation(prob[b][:], negc[b][:], ACT.Exp, bias=negm[b][:], scale=-1.0, accum_out=total[:, b : b + 1])
             for t in range(PACK):
                 nc.tensor.transpose(p_turned[b][:, t, :], prob[b][:, t * P : (t + 1) * P], ident[:])
 
         def token_scales(b):
             nc.vector.tensor_copy(vsg[b][:], window(vs_pool, b))
-            turned = psum.tile([P, PACK, P], F32, name="vs_turned%d" % b)
-            for t in range(PACK):
-                nc.tensor.transpose(turned[:, t, :], vsg[b][:, t::PACK], ident[:])
-            nc.scalar.copy(vs_col[b][:], turned[:, :, 0])
+            nc.sync.dma_start(out=vs_col[b][:], in_=vsg[b][0:1, :])
 
         def values(b):
             if b == 0:
                 nc.scalar.activation(vg[0][:], v0_bf[:].indirect(offsets[:, :COLS]), ACT.Copy)
             else:
                 nc.vector.tensor_copy(vg[1][:], window(v_pool, 1))
-            turned = psum.tile([P, 2, DV], F32, name="v_turned%d" % b)
+
+        def turn_values(b):
+            turned = psum.tile([P, 2, DV], F32, name="acc1" if b == 0 else "p_turned0")
             pairs = vg[b][:].bitcast(F32)
             for u in range(2):
                 nc.tensor.transpose(turned[:, u, :], pairs[:, u::2], ident[:])
             nc.scalar.copy(
-                v_il[b][:].rearrange("p e t -> p (e t)").bitcast(F32).rearrange("p (e u) -> p e u", u=2),
+                flat(v_il[b]).bitcast(F32).rearrange("p (e u) -> p e u", u=2),
                 turned[:].rearrange("p u e -> p e u"),
             )
 
@@ -166,9 +182,12 @@ def tile_attend_cap_sink_seg_kernel(tc, qT, k_words, k_scales, vT, vs, sink, off
                 w_il[b][:], p_turned[b][:].rearrange("p t q -> p q t"),
                 vs_col[b][:].unsqueeze(1).to_broadcast([P, NQ, PACK]), ALU.mult,
             )
-            quantize(v_codes[b], v_scales[b], v_il[b])
-            nc.vector.reciprocal(inv[b][:], total[b][:])
-            quantize(w_codes[b], w_scales[b], w_il[b])
+
+        def quantize_weights(b):
+            quantize(w_codes[b], w_scales[b], flat(w_il[b]))
+
+        def quantize_values(b):
+            quantize(v_codes[b], v_scales[b], flat(v_il[b]))
 
         def finish(b):
             y = psum.tile([P, DV], F32, name="acc%d" % b)
@@ -176,26 +195,37 @@ def tile_attend_cap_sink_seg_kernel(tc, qT, k_words, k_scales, vT, vs, sink, off
                 out=y[:], lhsT=w_codes[b][:].bitcast(FP8X4), lhsT_scale=w_scales[b][:],
                 rhs=v_codes[b][:].bitcast(FP8X4), rhs_scale=v_scales[b][:], start=True, stop=True,
             )
-            nc.scalar.activation(res[b][:], y[:], ACT.Copy, scale=inv[b][:])
+            nc.scalar.activation(res[b][:], y[:], ACT.Copy, scale=inv[:, b : b + 1])
             nc.sync.dma_start(out=out[b], in_=res[b][:])
 
         nc.vector.tensor_copy(ks[:], ks_pool[:].indirect(offsets[:]))
         queries(0)
         queries(1)
         keys(0)
+        quantize(q_codes, q_scales, q_il[:].rearrange("p b q j -> p (b q j)"))
+        token_scales(0)
+        sink_column(0)
+        sink_column(1)
+        for part in v0_parts:
+            nc.scalar.activation(v0_bf[:, part], v_pool[:, part], ACT.Copy)
         scores(0)
         keys(1)
+        values(0)
         scores(1)
         row_max(0)
+        token_scales(1)
         softmax(0)
-        token_scales(0)
-        nc.scalar.activation(v0_bf[:], v_pool[:, seg(0)], ACT.Copy)
         row_max(1)
         softmax(1)
-        token_scales(1)
-        values(0)
+        turn_values(0)
         values(1)
         weights(0)
-        finish(0)
+        turn_values(1)
+        quantize_values(0)
         weights(1)
+        quantize_weights(0)
+        nc.vector.reciprocal(inv[:], total[:])
+        quantize_weights(1)
+        quantize_values(1)
+        finish(0)
         finish(1)

@@ -46,10 +46,8 @@ def tile_attend_cap_sink_seg_kernel(tc, qT, k_words, k_scales, vT, vs, sink, off
         v_pool = sb("v_pool", [P, T], F32)
         vs_pool = sb("vs_pool", [P, T], F32)
         v0_bf = sb("v0_bf", [P, SEG], BF16)
-        sink_sb = sb("sink_sb", [P, B], F32)
+        sink_sb = per_seq("sink_sb", [P, 1], F32)
         ident = sb("ident", [P, P], F32)
-        warm = sb("warm", [P, 1], F32)
-        warm_out = sb("warm_out", [P, 1], F32)
         q_raw = sb("q_raw", [P, B, PACK, NQ], F32)
         q_il = sb("q_il", [P, B, NQ, PACK], BF16)
         q_codes = sb("q_codes", [P, B * NQ], U32)
@@ -66,6 +64,7 @@ def tile_attend_cap_sink_seg_kernel(tc, qT, k_words, k_scales, vT, vs, sink, off
         v_scales = per_seq("v_scales", [P, DV], U8)
         prob = per_seq("prob", [P, N + 1], F32)
         negm = per_seq("negm", [P, 1], F32)
+        part_sum = sb("part_sum", [P, 2, B], F32)
         total = sb("total", [P, B], F32)
         inv = sb("inv", [P, B], F32)
         w_il = per_seq("w_il", [P, NQ, PACK], BF16)
@@ -83,7 +82,6 @@ def tile_attend_cap_sink_seg_kernel(tc, qT, k_words, k_scales, vT, vs, sink, off
 
         nc.vector.memset(ks_pool[:, :SEG].bitcast(I32), 0)
         nc.gpsimd.memset(ks_pool[:, SEG:].bitcast(I32), 0)
-        nc.vector.memset(warm[:], 0.0)
         nc.vector.memset(ident[:], 0.0)
         for b in range(B):
             nc.vector.memset(vs_pool[:, seg(b)].bitcast(I32), 0)
@@ -96,13 +94,16 @@ def tile_attend_cap_sink_seg_kernel(tc, qT, k_words, k_scales, vT, vs, sink, off
                 out=ks_pool[32 * quad : 32 * quad + 4, :].bitcast(I32),
                 in_=k_scales[0, 4 * quad : 4 * quad + 4, :].bitcast(I32),
             )
-        nc.scalar.activation(warm_out[:], warm[:], ACT.Exp)
 
         def load_words(b):
             nc.sync.dma_start(
                 out=kw_pool[:, seg(b)].bitcast(I32),
                 in_=words[:, b * SEG * PACK : (b + 1) * SEG * PACK].bitcast(I32),
             )
+
+        def load_sink(b):
+            with nc.allow_non_contiguous_dma(reason="one sink logit a partition"):
+                nc.sync.dma_start(out=sink_sb[b][:], in_=sink[b])
 
         nc.sync.dma_start(
             out=q_raw[:].rearrange("p b j q -> p b (j q)"),
@@ -114,9 +115,9 @@ def tile_attend_cap_sink_seg_kernel(tc, qT, k_words, k_scales, vT, vs, sink, off
             nc.sync.dma_start(out=v_pool[:, part], in_=vT[:, part])
         nc.sync.dma_start(out=vs_pool[0:1, seg(0)], in_=vs[0:1, seg(0)])
         load_words(1)
+        load_sink(0)
         nc.sync.dma_start(out=vs_pool[0:1, seg(1)], in_=vs[0:1, seg(1)])
-        with nc.allow_non_contiguous_dma(reason="one sink logit a partition and sequence"):
-            nc.sync.dma_start(out=sink_sb[:], in_=sink.rearrange("b q o -> q (b o)"))
+        load_sink(1)
         nc.sync.dma_start(out=v_pool[:, seg(1)], in_=vT[:, seg(1)])
 
         def quantize(codes, scales, src):
@@ -126,26 +127,37 @@ def tile_attend_cap_sink_seg_kernel(tc, qT, k_words, k_scales, vT, vs, sink, off
             return tile3[:].rearrange("p c t -> p (c t)")
 
         def sink_column(b):
-            nc.gpsimd.tensor_scalar(half[b][:, N : N + 1], sink_sb[:, b : b + 1], 1.0 / CAP, 0.0, ALU.mult, ALU.add)
+            nc.gpsimd.tensor_scalar(half[b][:, N : N + 1], sink_sb[b][:], 1.0 / CAP, 0.0, ALU.mult, ALU.add)
 
         def queries(b):
             nc.scalar.activation(q_il[:, b], q_raw[:, b].rearrange("p j q -> p q j"), ACT.Copy)
 
+        pieces = (1, 2)
+
         def keys(b):
-            nc.vector.tensor_copy(kw[b][:], window(kw_pool, b))
+            n = N // pieces[b]
+            for i in range(pieces[b]):
+                first = b * COLS + i * n // 16
+                nc.vector.tensor_copy(
+                    kw[b][:, i * n : (i + 1) * n],
+                    kw_pool[:, : (b + 1) * SEG].indirect(offsets[:, first : first + n // 16]),
+                )
 
         def scores(b):
-            acc = psum.tile([P, N], F32, name="acc%d" % b)
+            n = N // pieces[b]
             cols = slice(b * NQ, (b + 1) * NQ)
-            nc.tensor.matmul_mx(
-                out=acc[:], lhsT=q_codes[:, cols].bitcast(FP8X4), lhsT_scale=q_scales[:, cols],
-                rhs=kw[b][:].bitcast(FP8X4), rhs_scale=ks[:, b * N : (b + 1) * N], start=True, stop=True,
-            )
-            nc.scalar.activation(
-                half[b][:, :N].rearrange("q (t s) -> q t s", t=PACK),
-                acc[:].rearrange("q (s t) -> q t s", t=PACK),
-                ACT.Tanh, scale=1.0 / CAP,
-            )
+            for i in range(pieces[b]):
+                acc = psum.tile([P, n], F32, name="acc%d" % (b + pieces[b] - 1 - i))
+                nc.tensor.matmul_mx(
+                    out=acc[:], lhsT=q_codes[:, cols].bitcast(FP8X4), lhsT_scale=q_scales[:, cols],
+                    rhs=kw[b][:, i * n : (i + 1) * n].bitcast(FP8X4),
+                    rhs_scale=ks[:, b * N + i * n : b * N + (i + 1) * n], start=True, stop=True,
+                )
+                nc.scalar.activation(
+                    half[b][:, :N].rearrange("q (t s) -> q t s", t=PACK)[:, :, i * n // PACK : (i + 1) * n // PACK],
+                    acc[:].rearrange("q (s t) -> q t s", t=PACK),
+                    ACT.Tanh, scale=1.0 / CAP,
+                )
 
         def row_max(b):
             nc.vector.tensor_scalar(negc[b][:], half[b][:], -CAP, None, ALU.mult, ALU.min, accum_out=negm[b][:])
@@ -153,9 +165,13 @@ def tile_attend_cap_sink_seg_kernel(tc, qT, k_words, k_scales, vT, vs, sink, off
         p_turned = [psum.tile([P, PACK, NQ], F32, name="p_turned%d" % b) for b in range(B)]
 
         def softmax(b):
-            nc.scalar.activation(prob[b][:], negc[b][:], ACT.Exp, bias=negm[b][:], scale=-1.0, accum_out=total[:, b : b + 1])
-            for t in range(PACK):
-                nc.tensor.transpose(p_turned[b][:, t, :], prob[b][:, t * P : (t + 1) * P], ident[:])
+            for h, cols in enumerate((slice(0, N // 2), slice(N // 2, N + 1))):
+                nc.scalar.activation(
+                    prob[b][:, cols], negc[b][:, cols], ACT.Exp, bias=negm[b][:], scale=-1.0,
+                    accum_out=part_sum[:, h, b : b + 1],
+                )
+                for t in (2 * h, 2 * h + 1):
+                    nc.tensor.transpose(p_turned[b][:, t, :], prob[b][:, t * P : (t + 1) * P], ident[:])
 
         def token_scales(b):
             nc.vector.tensor_copy(vsg[b][:], window(vs_pool, b))
@@ -168,7 +184,7 @@ def tile_attend_cap_sink_seg_kernel(tc, qT, k_words, k_scales, vT, vs, sink, off
                 nc.vector.tensor_copy(vg[1][:], window(v_pool, 1))
 
         def turn_values(b):
-            turned = psum.tile([P, 2, DV], F32, name="acc1" if b == 0 else "p_turned0")
+            turned = psum.tile([P, 2, DV], F32, name="acc1")
             pairs = vg[b][:].bitcast(F32)
             for u in range(2):
                 nc.tensor.transpose(turned[:, u, :], pairs[:, u::2], ident[:])
@@ -219,11 +235,12 @@ def tile_attend_cap_sink_seg_kernel(tc, qT, k_words, k_scales, vT, vs, sink, off
         softmax(1)
         turn_values(0)
         values(1)
-        weights(0)
         turn_values(1)
+        weights(0)
         quantize_values(0)
-        weights(1)
         quantize_weights(0)
+        weights(1)
+        nc.gpsimd.tensor_tensor(total[:], part_sum[:, 0, :], part_sum[:, 1, :], ALU.add)
         nc.vector.reciprocal(inv[:], total[:])
         quantize_weights(1)
         quantize_values(1)

@@ -39,22 +39,23 @@ def tile_attend_cap_sink_seg_kernel(tc, qT, k_words, k_scales, vT, vs, sink, off
         def per_seq(name, shape, dtype):
             return [sb("%s%d" % (name, b), shape, dtype) for b in range(B)]
 
-        KW = 0
+        KW, V0 = 0, 4096
         offsets = keep.tile([P, B * COLS], U16, name="offsets")
         kw_pool = sb("kw_pool", [P, T], U32)
         ks_pool = sb("ks_pool", [P, T], U8)
         v_pool = sb("v_pool", [P, T], F32)
         vs_pool = sb("vs_pool", [P, T], F32)
+        v0_raw = at(V0, "v0_raw", [P, SEG], F32)
         v0_bf = sb("v0_bf", [P, SEG], BF16)
         sink_sb = per_seq("sink_sb", [P, 1], F32)
         ident = sb("ident", [P, P], F32)
-        q_raw = sb("q_raw", [P, B, PACK, NQ], F32)
-        q_il = sb("q_il", [P, B, NQ, PACK], BF16)
+        q_raw = per_seq("q_raw", [P, PACK, NQ], F32)
+        q_il = per_seq("q_il", [P, NQ, PACK], BF16)
         q_codes = sb("q_codes", [P, B * NQ], U32)
         q_scales = sb("q_scales", [P, B * NQ], U8)
         kw = per_seq("kw", [P, N], U32)
         ks = sb("ks", [P, B * N], U8)
-        half = per_seq("half", [P, N + 1], F32)
+        half = [at(V0, "half0", [P, N + 1], F32), sb("half1", [P, N + 1], F32)]
         negc = [sb("negc0", [P, N + 1], F32), at(KW, "negc1", [P, N + 1], F32)]
         vsg = per_seq("vsg", [P, N], F32)
         vg = per_seq("vg", [P, N], BF16)
@@ -83,8 +84,9 @@ def tile_attend_cap_sink_seg_kernel(tc, qT, k_words, k_scales, vT, vs, sink, off
         nc.vector.memset(ks_pool[:, :SEG].bitcast(I32), 0)
         nc.gpsimd.memset(ks_pool[:, SEG:].bitcast(I32), 0)
         nc.vector.memset(ident[:], 0.0)
-        for b in range(B):
-            nc.vector.memset(vs_pool[:, seg(b)].bitcast(I32), 0)
+        nc.vector.memset(vs_pool[:, seg(0)].bitcast(I32), 0)
+        nc.vector.memset(v_pool[:, seg(0)].bitcast(I32), 0)
+        nc.vector.memset(vs_pool[:, seg(1)].bitcast(I32), 0)
         make_identity(nc, ident[:], nomemset=True)
 
         nc.sync.dma_start(offsets[:], offs)
@@ -105,14 +107,13 @@ def tile_attend_cap_sink_seg_kernel(tc, qT, k_words, k_scales, vT, vs, sink, off
             with nc.allow_non_contiguous_dma(reason="one sink logit a partition"):
                 nc.sync.dma_start(out=sink_sb[b][:], in_=sink[b])
 
-        nc.sync.dma_start(
-            out=q_raw[:].rearrange("p b j q -> p b (j q)"),
-            in_=qT.rearrange("b (p j) q -> p b (j q)", j=PACK),
-        )
+        def load_queries(b):
+            nc.sync.dma_start(out=q_raw[b][:], in_=qT[b].rearrange("(p j) q -> p j q", j=PACK))
+
+        load_queries(0)
         load_words(0)
-        v0_parts = (slice(0, 768), slice(768, SEG))
-        for part in v0_parts:
-            nc.sync.dma_start(out=v_pool[:, part], in_=vT[:, part])
+        load_queries(1)
+        nc.sync.dma_start(out=v0_raw[:], in_=vT[:, seg(0)])
         nc.sync.dma_start(out=vs_pool[0:1, seg(0)], in_=vs[0:1, seg(0)])
         load_words(1)
         load_sink(0)
@@ -130,7 +131,9 @@ def tile_attend_cap_sink_seg_kernel(tc, qT, k_words, k_scales, vT, vs, sink, off
             nc.gpsimd.tensor_scalar(half[b][:, N : N + 1], sink_sb[b][:], 1.0 / CAP, 0.0, ALU.mult, ALU.add)
 
         def queries(b):
-            nc.scalar.activation(q_il[:, b], q_raw[:, b].rearrange("p j q -> p q j"), ACT.Copy)
+            nc.scalar.activation(q_il[b][:], q_raw[b][:].rearrange("p j q -> p q j"), ACT.Copy)
+            cols = slice(b * NQ, (b + 1) * NQ)
+            quantize(q_codes[:, cols], q_scales[:, cols], flat(q_il[b]))
 
         pieces = (1, 2)
 
@@ -216,14 +219,12 @@ def tile_attend_cap_sink_seg_kernel(tc, qT, k_words, k_scales, vT, vs, sink, off
 
         nc.vector.tensor_copy(ks[:], ks_pool[:].indirect(offsets[:]))
         queries(0)
-        queries(1)
         keys(0)
-        quantize(q_codes, q_scales, q_il[:].rearrange("p b q j -> p (b q j)"))
+        queries(1)
         token_scales(0)
+        nc.scalar.activation(v0_bf[:], v0_raw[:], ACT.Copy)
         sink_column(0)
         sink_column(1)
-        for part in v0_parts:
-            nc.scalar.activation(v0_bf[:, part], v_pool[:, part], ACT.Copy)
         scores(0)
         keys(1)
         values(0)
@@ -240,7 +241,8 @@ def tile_attend_cap_sink_seg_kernel(tc, qT, k_words, k_scales, vT, vs, sink, off
         quantize_values(0)
         quantize_weights(0)
         weights(1)
-        nc.gpsimd.tensor_tensor(total[:], part_sum[:, 0, :], part_sum[:, 1, :], ALU.add)
+        for b in range(B):
+            nc.scalar.activation(total[:, b : b + 1], part_sum[:, 0, b : b + 1], ACT.Identity, bias=part_sum[:, 1, b : b + 1])
         nc.vector.reciprocal(inv[:], total[:])
         quantize_weights(1)
         quantize_values(1)

from contextlib import ExitStack

import concourse.mybir as mybir
from concourse.masks import make_identity

B, N, T, D, DV, NQ = 2, 512, 2048, 512, 128, 128
CAP = 2.0
FLOPS = 2 * B * NQ * N * (D + DV)

F32 = mybir.dt.float32
BF16 = mybir.dt.bfloat16
I32 = mybir.dt.int32
U32 = mybir.dt.uint32
U16 = mybir.dt.uint16
U8 = mybir.dt.uint8
FP8X4 = mybir.dt.float8_e4m3fn_x4
ACT = mybir.ActivationFunctionType
ALU = mybir.AluOpType

P = 128
PACK = 4
SEG = T // B
COLS = N // 16


def tile_attend_cap_sink_seg_kernel(tc, qT, k_words, k_scales, vT, vs, sink, offs, out):
    nc = tc.nc
    with ExitStack() as ctx:
        keep = ctx.enter_context(tc.tile_pool(name="keep", bufs=1))
        psum = ctx.enter_context(tc.psum_pool(name="psum", bufs=1))
        reuse = ctx.enter_context(tc.tile_pool(name="reuse", bufs=1))

        def sb(name, shape, dtype):
            return keep.tile(shape, dtype, name=name, align_bytes=64)

        def at(offset, name, shape, dtype):
            return reuse.tile(shape, dtype, name=name, align_bytes=64, offset=offset)

        def per_seq(name, shape, dtype):
            return [sb("%s%d" % (name, b), shape, dtype) for b in range(B)]

        KW, V0 = 0, 4096
        offsets = keep.tile([P, B * COLS], U16, name="offsets")
        kw_pool = sb("kw_pool", [P, T], U32)
        ks_pool = sb("ks_pool", [P, T], U8)
        v_pool = sb("v_pool", [P, T], F32)
        vs_pool = sb("vs_pool", [P, T], F32)
        v0_raw = at(V0, "v0_raw", [P, SEG], F32)
        v0_bf = sb("v0_bf", [P, SEG], BF16)
        sink_sb = per_seq("sink_sb", [P, 1], F32)
        ident = sb("ident", [P, P], F32)
        q_raw = per_seq("q_raw", [P, PACK, NQ], F32)
        q_il = per_seq("q_il", [P, NQ, PACK], BF16)
        q_codes = sb("q_codes", [P, B * NQ], U32)
        q_scales = sb("q_scales", [P, B * NQ], U8)
        kw = per_seq("kw", [P, N], U32)
        ks = sb("ks", [P, B * N], U8)
        half = [at(V0, "half0", [P, N + 1], F32), sb("half1", [P, N + 1], F32)]
        negc = [sb("negc0", [P, N + 1], F32), at(KW, "negc1", [P, N + 1], F32)]
        vsg = per_seq("vsg", [P, N], F32)
        vg = per_seq("vg", [P, N], BF16)
        vs_col = per_seq("vs_col", [P, PACK], F32)
        v_il = [at(KW, "v_il0", [P, DV, PACK], BF16), sb("v_il1", [P, DV, PACK], BF16)]
        v_codes = per_seq("v_codes", [P, DV], U32)
        v_scales = per_seq("v_scales", [P, DV], U8)
        prob = per_seq("prob", [P, N + 1], F32)
        negm = per_seq("negm", [P, 1], F32)
        part_sum = sb("part_sum", [P, 2, B], F32)
        total = sb("total", [P, B], F32)
        inv = sb("inv", [P, B], F32)
        w_il = per_seq("w_il", [P, NQ, PACK], BF16)
        w_codes = per_seq("w_codes", [P, NQ], U32)
        w_scales = per_seq("w_scales", [P, NQ], U8)
        res = per_seq("res", [P, DV], F32)

        def seg(b):
            return slice(b * SEG, (b + 1) * SEG)

        def window(pool_tile, b):
            return pool_tile[:, : (b + 1) * SEG].indirect(offsets[:, b * COLS : (b + 1) * COLS])

        words = k_words[0].rearrange("p n t -> p (n t)")

        nc.vector.memset(ks_pool[:, :SEG].bitcast(I32), 0)
        nc.gpsimd.memset(ks_pool[:, SEG:].bitcast(I32), 0)
        nc.vector.memset(ident[:], 0.0)
        nc.vector.memset(vs_pool[:, seg(0)].bitcast(I32), 0)
        nc.vector.memset(v_pool[:, seg(0)].bitcast(I32), 0)
        nc.vector.memset(vs_pool[:, seg(1)].bitcast(I32), 0)
        make_identity(nc, ident[:], nomemset=True)

        nc.sync.dma_start(offsets[:], offs)
        for quad in range(4):
            queue = nc.sync if quad < 2 else nc.scalar
            queue.dma_start(
                out=ks_pool[32 * quad : 32 * quad + 4, :].bitcast(I32),
                in_=k_scales[0, 4 * quad : 4 * quad + 4, :].bitcast(I32),
            )

        def load_words(b):
            nc.sync.dma_start(
                out=kw_pool[:, seg(b)].bitcast(I32),
                in_=words[:, b * SEG * PACK : (b + 1) * SEG * PACK].bitcast(I32),
            )

        def load_sink(b):
            with nc.allow_non_contiguous_dma(reason="one sink logit a partition"):
                nc.sync.dma_start(out=sink_sb[b][:], in_=sink[b])

        def load_queries(b):
            nc.sync.dma_start(out=q_raw[b][:], in_=qT[b].rearrange("(p j) q -> p j q", j=PACK))

        load_queries(0)
        load_words(0)
        load_queries(1)
        nc.sync.dma_start(out=v0_raw[:], in_=vT[:, seg(0)])
        nc.sync.dma_start(out=vs_pool[0:1, seg(0)], in_=vs[0:1, seg(0)])
        load_words(1)
        load_sink(0)
        nc.sync.dma_start(out=vs_pool[0:1, seg(1)], in_=vs[0:1, seg(1)])
        load_sink(1)
        nc.sync.dma_start(out=v_pool[:, seg(1)], in_=vT[:, seg(1)])

        def quantize(codes, scales, src):
            nc.vector.quantize_mx(out=codes[:].bitcast(FP8X4), scales=scales[:], in_=src)

        def flat(tile3):
            return tile3[:].rearrange("p c t -> p (c t)")

        def sink_column(b):
            nc.gpsimd.tensor_scalar(half[b][:, N : N + 1], sink_sb[b][:], 1.0 / CAP, 0.0, ALU.mult, ALU.add)

        def queries(b):
            nc.scalar.activation(q_il[b][:], q_raw[b][:].rearrange("p j q -> p q j"), ACT.Copy)
            cols = slice(b * NQ, (b + 1) * NQ)
            quantize(q_codes[:, cols], q_scales[:, cols], flat(q_il[b]))

        pieces = (1, 2)

        def keys(b):
            n = N // pieces[b]
            for i in range(pieces[b]):
                first = b * COLS + i * n // 16
                nc.vector.tensor_copy(
                    kw[b][:, i * n : (i + 1) * n],
                    kw_pool[:, : (b + 1) * SEG].indirect(offsets[:, first : first + n // 16]),
                )

        def scores(b):
            n = N // pieces[b]
            cols = slice(b * NQ, (b + 1) * NQ)
            for i in range(pieces[b]):
                acc = psum.tile([P, n], F32, name="acc%d" % (b + pieces[b] - 1 - i))
                nc.tensor.matmul_mx(
                    out=acc[:], lhsT=q_codes[:, cols].bitcast(FP8X4), lhsT_scale=q_scales[:, cols],
                    rhs=kw[b][:, i * n : (i + 1) * n].bitcast(FP8X4),
                    rhs_scale=ks[:, b * N + i * n : b * N + (i + 1) * n], start=True, stop=True,
                )
                nc.scalar.activation(
                    half[b][:, :N].rearrange("q (t s) -> q t s", t=PACK)[:, :, i * n // PACK : (i + 1) * n // PACK],
                    acc[:].rearrange("q (s t) -> q t s", t=PACK),
                    ACT.Tanh, scale=1.0 / CAP,
                )

        def row_max(b):
            nc.vector.tensor_scalar(negc[b][:], half[b][:], -CAP, None, ALU.mult, ALU.min, accum_out=negm[b][:])

        p_turned = [psum.tile([P, PACK, NQ], F32, name="p_turned%d" % b) for b in range(B)]

        def softmax(b):
            for h, cols in enumerate((slice(0, N // 2), slice(N // 2, N + 1))):
                nc.scalar.activation(
                    prob[b][:, cols], negc[b][:, cols], ACT.Exp, bias=negm[b][:], scale=-1.0,
                    accum_out=part_sum[:, h, b : b + 1],
                )
                for t in (2 * h, 2 * h + 1):
                    nc.tensor.transpose(p_turned[b][:, t, :], prob[b][:, t * P : (t + 1) * P], ident[:])

        def token_scales(b):
            nc.vector.tensor_copy(vsg[b][:], window(vs_pool, b))
            nc.sync.dma_start(out=vs_col[b][:], in_=vsg[b][0:1, :])

        def values(b):
            if b == 0:
                nc.scalar.activation(vg[0][:], v0_bf[:].indirect(offsets[:, :COLS]), ACT.Copy)
            else:
                nc.vector.tensor_copy(vg[1][:], window(v_pool, 1))

        def turn_values(b):
            turned = psum.tile([P, 2, DV], F32, name="acc1")
            pairs = vg[b][:].bitcast(F32)
            for u in range(2):
                nc.tensor.transpose(turned[:, u, :], pairs[:, u::2], ident[:])
            nc.scalar.copy(
                flat(v_il[b]).bitcast(F32).rearrange("p (e u) -> p e u", u=2),
                turned[:].rearrange("p u e -> p e u"),
            )

        def weights(b):
            nc.vector.tensor_tensor(
                w_il[b][:], p_turned[b][:].rearrange("p t q -> p q t"),
                vs_col[b][:].unsqueeze(1).to_broadcast([P, NQ, PACK]), ALU.mult,
            )

        def quantize_weights(b):
            quantize(w_codes[b], w_scales[b], flat(w_il[b]))

        def quantize_values(b):
            quantize(v_codes[b], v_scales[b], flat(v_il[b]))

        def finish(b):
            y = psum.tile([P, DV], F32, name="acc%d" % b)
            nc.tensor.matmul_mx(
                out=y[:], lhsT=w_codes[b][:].bitcast(FP8X4), lhsT_scale=w_scales[b][:],
                rhs=v_codes[b][:].bitcast(FP8X4), rhs_scale=v_scales[b][:], start=True, stop=True,
            )
            nc.scalar.activation(res[b][:], y[:], ACT.Copy, scale=inv[:, b : b + 1])
            nc.sync.dma_start(out=out[b], in_=res[b][:])

        nc.vector.tensor_copy(ks[:], ks_pool[:].indirect(offsets[:]))
        queries(0)
        keys(0)
        queries(1)
        token_scales(0)
        nc.scalar.activation(v0_bf[:], v0_raw[:], ACT.Copy)
        sink_column(0)
        sink_column(1)
        scores(0)
        keys(1)
        values(0)
        scores(1)
        row_max(0)
        token_scales(1)
        softmax(0)
        row_max(1)
        softmax(1)
        turn_values(0)
        values(1)
        turn_values(1)
        weights(0)
        quantize_values(0)
        quantize_weights(0)
        weights(1)
        for b in range(B):
            nc.scalar.activation(total[:, b : b + 1], part_sum[:, 0, b : b + 1], ACT.Identity, bias=part_sum[:, 1, b : b + 1])
        nc.vector.reciprocal(inv[:], total[:])
        quantize_weights(1)
        quantize_values(1)
        finish(0)
        finish(1)
